import numpy as np
import ml_dtypes


def mxq(x, axis, fmt="e4m3"):
    dtype, down = {"e4m3": (ml_dtypes.float8_e4m3fn, 7), "e5m2": (ml_dtypes.float8_e5m2, 14)}[fmt]
    v = np.moveaxis(np.asarray(x, np.float32).astype(ml_dtypes.bfloat16).astype(np.float64), axis, -1)
    blocks = v.reshape(v.shape[:-1] + (-1, 32))
    amax = np.abs(blocks).max(-1, keepdims=True)
    byte = np.maximum(np.where(amax > 0, np.frexp(amax)[1] - 1 + 127, 0) - down, 1)
    scale = np.exp2(byte - 127.0)
    codes = (blocks / scale).astype(np.float32).astype(dtype).astype(np.float64)
    return np.moveaxis((codes * scale).reshape(v.shape), -1, axis)


WIDE = False


def mx_kscale(k):
    if not WIDE:
        return np.ones(k)
    levels = np.array([10, -10, 5, -5, 0])
    if k % 512:
        return np.exp2(np.random.permutation(np.resize(levels, k // 32))).repeat(32)
    a = np.empty((k // 512, 16))
    for p in range(k // 512):
        a[p, :8] = np.random.permutation(np.resize(levels, 8))
        for g in range(8):
            far = levels[np.abs(levels - a[p, g]) >= 10]
            a[p, g + 8] = far[np.random.randint(len(far))]
    return np.exp2(a.ravel()).repeat(32)


def f64(x):
    return np.asarray(x).astype(np.float64)


def striped(idx):
    return np.tile(idx.reshape(-1, 16).T, (8, 1)).astype(np.uint16)


def unstriped(offs):
    return offs[:16].T.reshape(-1).astype(np.int64)


def striped8(idx):
    return np.concatenate([x.reshape(-1, 16).T for x in idx]).astype(np.uint16)


def runs(offs, k):
    lists = np.stack([offs[16 * r : 16 * r + 16].T.reshape(-1) for r in range(8)]).astype(np.int64)
    return lists[np.arange(k) % 512 // 64]


def pack_weight(w):
    k, n = w.shape
    w = f64(np.asarray(w, np.float32).astype(ml_dtypes.bfloat16)).reshape(k // 32, 32, n)
    amax = np.abs(w).max(1)
    byte = np.clip(np.where(amax > 0, np.frexp(amax)[1] - 1 + 127 - 7, 1), 1, 254)
    scaled = (w * np.exp2(127.0 - byte)[:, None, :]).reshape(k, n).astype(np.float32)
    words = np.ascontiguousarray(scaled.reshape(k // 512, 128, 4, n).transpose(0, 1, 3, 2)).astype(ml_dtypes.float8_e4m3fn).view(np.uint8)
    return words, np.ascontiguousarray(byte.astype(np.uint8).reshape(k // 512, 16, n))


def unpack_weight(words, scales):
    g, p, n, _ = words.shape
    vals = np.ascontiguousarray(words).view(ml_dtypes.float8_e4m3fn).astype(np.float64) * np.repeat(np.exp2(scales.astype(np.float64) - 127.0), 8, axis=1)[..., None]
    return vals.transpose(0, 1, 3, 2).reshape(g * 512, n)


def sigmoid(v):
    return 1.0 / (1.0 + np.exp(-np.maximum(v, -700.0)))


K, T, S, N, G, H, W = 512, 1024, 256, 512, 2048, 512, 128


def setup_inputs():
    n = np.random.standard_normal
    s = mx_kscale(K)[:, None]
    u = mx_kscale(K)
    packed_xT = pack_weight(n((K, T)) * s)
    packed_dT = pack_weight(n((K, G)) / s)
    packed_w1 = pack_weight(n((H, N)) / np.sqrt(2 * H) / u[:, None])
    packed_w2 = pack_weight(n((K, N)) / np.sqrt(2 * K) / s)
    perm = np.random.permutation(S)
    perm2 = np.random.permutation(S)
    perm3 = np.random.permutation(S)
    perm4 = np.random.permutation(S)
    return {
        "x_words": packed_xT[0],
        "x_scales": packed_xT[1],
        "d_words": packed_dT[0],
        "d_scales": packed_dT[1],
        "gn": (np.random.uniform(0.5, 1.5, (H, 1)) * u[:, None]).astype(np.float32),
        "w1_words": packed_w1[0],
        "w1_scales": packed_w1[1],
        "w2_words": packed_w2[0],
        "w2_scales": packed_w2[1],
        "sl": np.random.uniform(1.0, 2.0, (N, 1)).astype(np.float32),
        "th": (0.5 * n((N, 1))).astype(np.float32),
        "offs": striped(np.random.permutation(T)[:S]),
        "k1": striped8(np.random.randint(0, G, (8, H))),
        "two": striped(np.random.permutation(T)[:S]),
        "k2": striped8(np.random.randint(0, G, (8, H))),
        "n1": striped(perm[:W]),
        "n2": striped(perm[W:]),
        "n3": striped(perm2[:W]),
        "n4": striped(perm2[W:]),
        "n5": striped(np.random.permutation(S)),
        "duo": striped(np.random.permutation(T)[:S]),
        "n6": striped(perm3[:W]),
        "n7": striped(perm3[W:]),
        "n8": striped(perm4[:W]),
        "n9": striped(perm4[W:]),
        "n10": striped(np.random.permutation(S)),
    }


def reference(x_words, x_scales, d_words, d_scales, gn, w1_words, w1_scales, w2_words, w2_scales, sl, th, offs, k1, two, k2, n1, n2, n3, n4, n5, duo, n6, n7, n8, n9, n10):
    d_k1 = unpack_weight(d_words, d_scales)[np.arange(K)[:, None], runs(k1, K)]
    xq = unpack_weight(x_words, x_scales)[:, unstriped(offs)]
    d_k2 = unpack_weight(d_words, d_scales)[np.arange(K)[:, None], runs(k2, K)]
    x_two = unpack_weight(x_words, x_scales)[:, unstriped(two)]
    h = 0.0625 * (d_k1.T @ xq + d_k2.T @ x_two)
    pa = h[:, unstriped(n1)]
    pb = h[:, unstriped(n2)]
    rb = pa + pb
    ra = np.minimum(pa, pb)
    ua = np.zeros((H, S))
    ua[:, unstriped(n3)] = ra
    ub = ua.copy()
    ub[:, unstriped(n4)] = rb
    ds = np.zeros((H, S))
    ds[:, unstriped(n5)] = ub
    z = f64(gn) * (ub - ds)
    x_duo = unpack_weight(x_words, x_scales)[:, unstriped(duo)]
    h2 = unpack_weight(w1_words, w1_scales).T @ mxq(z, 0, "e4m3") + unpack_weight(w2_words, w2_scales).T @ x_duo
    pa2 = h2[:, unstriped(n6)]
    pb2 = h2[:, unstriped(n7)]
    rb2 = np.minimum(pa2, pb2)
    ra2 = np.maximum(pa2, pb2)
    ua2 = np.zeros((N, S))
    ua2[:, unstriped(n8)] = ra2
    ub2 = ua2.copy()
    ub2[:, unstriped(n9)] = rb2
    sg = sigmoid(f64(sl) * (ub2[:, unstriped(n10)] - f64(th)))
    return ub2 * sg

@@ -1,0 +1,209 @@
+from contextlib import ExitStack
+
+import concourse.mybir as mybir
+
+K, T, S, N, G, H, W = 512, 1024, 256, 512, 2048, 512, 128
+FLOPS = 2 * 4 * 512 * 512 * 256
+
+F32 = mybir.dt.float32
+BF16 = mybir.dt.bfloat16
+I32 = mybir.dt.int32
+U32 = mybir.dt.uint32
+U16 = mybir.dt.uint16
+U8 = mybir.dt.uint8
+FP8X4 = mybir.dt.float8_e4m3fn_x4
+ACT = mybir.ActivationFunctionType
+ALU = mybir.AluOpType
+
+P = 128
+PACK = 4
+TILES = 4
+WIDE = 2 * S
+
+
+def tile_picked_mttzntcpsdeord_none_p_kernel(
+    tc, x_words, x_scales, d_words, d_scales, gn, w1_words, w1_scales, w2_words, w2_scales, sl, th,
+    offs, k1, two, k2, n1, n2, n3, n4, n5, duo, n6, n7, n8, n9, n10, out,
+):
+    nc = tc.nc
+
+    with ExitStack() as ctx:
+        keep = ctx.enter_context(tc.tile_pool(name="keep", bufs=1))
+        psum = ctx.enter_context(tc.psum_pool(name="psum", bufs=1))
+
+        def load_list(src, name):
+            tile = keep.tile(list(src.shape), U16, name=name)
+            nc.sync.dma_start(tile[:], src)
+            return tile
+
+        def load_words(src, name, tag=""):
+            tile = keep.tile([P, src.shape[2]], U32, name=name, tag=tag or name, align_bytes=64)
+            nc.sync.dma_start(tile[:].bitcast(I32), src[0].rearrange("p n r -> p (n r)").bitcast(I32))
+            return tile
+
+        def zeroed_bytes(width, name):
+            tile = keep.tile([P, width], U8, name=name, align_bytes=64)
+            nc.vector.memset(tile[:].bitcast(I32), 0)
+            return tile
+
+        def load_scale_rows(tile, src, queue):
+            rows = src[0].bitcast(I32)
+            for r in range(4):
+                queue.dma_start(tile[r:P:32, :].bitcast(I32), rows[r:16:4, :])
+
+        d_bytes = zeroed_bytes(G, "d_bytes")
+        x_bytes = zeroed_bytes(T, "x_bytes")
+        dk_plane = zeroed_bytes(2 * H, "dk_plane")
+        k1_t = load_list(k1, "k1")
+        k2_t = load_list(k2, "k2")
+        nc.scalar.dma_start(d_bytes[0:P:8, :].bitcast(I32), d_scales[0].bitcast(I32))
+        d_tab = load_words(d_words, "d_tab")
+        offs_t = load_list(offs, "offs")
+        two_t = load_list(two, "two")
+        x_tab = load_words(x_words, "x_tab")
+        load_scale_rows(x_bytes, x_scales, nc.scalar)
+
+        dk_bytes = keep.tile([P, 2 * H], U8, name="dk_bytes", align_bytes=64)
+        for l, lst in enumerate((k1_t, k2_t)):
+            nc.vector.tensor_copy(dk_bytes[:, l * H : (l + 1) * H], d_bytes[:].indirect(lst[:]))
+        for r in range(4):
+            nc.scalar.dma_start(dk_plane[r:P:32, :].bitcast(I32), dk_bytes[8 * r : P : 32, :].bitcast(I32))
+        dk_words = keep.tile([P, 2 * H], U32, name="dk_words", tag="picked", align_bytes=64)
+        for l, lst in enumerate((k1_t, k2_t)):
+            nc.vector.tensor_copy(dk_words[:, l * H : (l + 1) * H], d_tab[:].indirect(lst[:]))
+        xq_words = keep.tile([P, 2 * S], U32, name="xq_words", align_bytes=64)
+        xq_plane = keep.tile([P, 2 * S], U8, name="xq_plane", align_bytes=64)
+        for l, lst in enumerate((offs_t, two_t)):
+            nc.vector.tensor_copy(xq_words[:, l * S : (l + 1) * S], x_tab[:].indirect(lst[:]))
+        for l, lst in enumerate((offs_t, two_t)):
+            nc.vector.tensor_copy(xq_plane[:, l * S : (l + 1) * S], x_bytes[:].indirect(lst[:]))
+
+        n1_t, n2_t, n3_t, n4_t, n5_t = [load_list(a, nm) for a, nm in ((n1, "n1"), (n2, "n2"), (n3, "n3"), (n4, "n4"), (n5, "n5"))]
+        gain = keep.tile([P, TILES], F32, name="gain")
+        nc.sync.dma_start(gain[:], gn.rearrange("(p t) o -> p (t o)", t=TILES))
+
+        h = []
+        for t in range(TILES):
+            lhs_words = keep.tile([P, 2, P], U32, name="lhs_words%d" % t, align_bytes=64)
+            lhs_plane = keep.tile([P, 2, P], U8, name="lhs_plane%d" % t, align_bytes=64)
+            nc.vector.tensor_copy(lhs_words[:], dk_words[:].rearrange("p (l m t) -> p t l m", l=2, t=TILES)[:, t])
+            nc.vector.tensor_copy(lhs_plane[:], dk_plane[:].rearrange("p (l m t) -> p t l m", l=2, t=TILES)[:, t])
+            acc = psum.tile([P, S], F32, name="h_acc%d" % t)
+            for l in range(2):
+                cols = slice(l * S, (l + 1) * S)
+                nc.tensor.matmul_mx(
+                    out=acc[:],
+                    lhsT=lhs_words[:, l, :].bitcast(FP8X4),
+                    lhsT_scale=lhs_plane[:, l, :],
+                    rhs=xq_words[:, cols].bitcast(FP8X4),
+                    rhs_scale=xq_plane[:, cols],
+                    start=(l == 0),
+                    stop=(l == 1),
+                )
+            h_t = keep.tile([P, S], F32, name="h%d" % t)
+            if t == 0:
+                nc.scalar.activation(h_t[:], acc[:], ACT.Copy, scale=0.0625)
+            else:
+                nc.vector.tensor_scalar(h_t[:], acc[:], 0.0625, None, ALU.mult)
+            h.append(h_t)
+
+        duo_t, n6_t, n7_t, n8_t, n9_t, n10_t = [load_list(a, nm) for a, nm in ((duo, "duo"), (n6, "n6"), (n7, "n7"), (n8, "n8"), (n9, "n9"), (n10, "n10"))]
+        w2_tab = load_words(w2_words, "w2_tab")
+        w1_tab = load_words(w1_words, "w1_tab")
+        w2_plane = zeroed_bytes(N, "w2_plane")
+        w1_plane = zeroed_bytes(N, "w1_plane")
+        load_scale_rows(w2_plane, w2_scales, nc.sync)
+        load_scale_rows(w1_plane, w1_scales, nc.sync)
+        slope = keep.tile([P, TILES], F32, name="slope")
+        thresh = keep.tile([P, TILES], F32, name="thresh")
+        with nc.allow_non_contiguous_dma(reason="one value a row"):
+            nc.sync.dma_start(slope[:], sl.rearrange("(t p) o -> p (t o)", t=TILES))
+            nc.sync.dma_start(thresh[:], th.rearrange("(t p) o -> p (t o)", t=TILES))
+
+        neg_gain = keep.tile([P, TILES], F32, name="neg_gain")
+        nc.vector.tensor_scalar(neg_gain[:], gain[:], -1.0, None, ALU.mult)
+        bias = keep.tile([P, TILES], F32, name="bias")
+        nc.vector.scalar_tensor_tensor(bias[:], slope[:], -1.0, thresh[:], ALU.mult, ALU.mult)
+
+        def pair_up(src, tiles, first, second, op_a, op_b, dst, put_a, put_b, name):
+            ra, rb = {}, {}
+            for t in tiles:
+                pa = keep.tile([P, W], F32, name="%s_pa%d" % (name, t))
+                pb = keep.tile([P, W], F32, name="%s_pb%d" % (name, t))
+                nc.scalar.activation(pa[:], src[t][:].indirect(first[:]), ACT.Copy)
+                nc.scalar.activation(pb[:], src[t][:].indirect(second[:]), ACT.Copy)
+                ra[t] = keep.tile([P, W], F32, name="%s_ra%d" % (name, t))
+                rb[t] = keep.tile([P, W], F32, name="%s_rb%d" % (name, t))
+                nc.vector.tensor_tensor(ra[t][:], pa[:], pb[:], op_a)
+                nc.vector.tensor_tensor(rb[t][:], pa[:], pb[:], op_b)
+            for t in tiles:
+                nc.scalar.activation(dst[t][:].indirect(put_a[:]), ra[t][:], ACT.Copy)
+            for t in tiles:
+                nc.scalar.activation(dst[t][:].indirect(put_b[:]), rb[t][:], ACT.Copy)
+
+        halves = [keep.tile([P, W, PACK], BF16, name="z_half%d" % c, align_bytes=64) for c in range(2)]
+        ub = [keep.tile([P, S], F32, name="ub%d" % t) for t in range(TILES)]
+        for tiles in ((0, 1), (2, 3)):
+            pair_up(h, tiles, n1_t, n2_t, ALU.min, ALU.add, ub, n3_t, n4_t, "a")
+            for t in tiles:
+                ds = keep.tile([P, WIDE], F32, name="ds%d" % t)
+                nc.scalar.activation(ds[:].indirect(n5_t[:]), ub[t][:], ACT.Copy)
+                gub = keep.tile([P, S], F32, name="gub%d" % t)
+                nc.vector.tensor_scalar(gub[:], ub[t][:], gain[:, t : t + 1], None, ALU.mult)
+                for c in range(2):
+                    cols = slice(c * W, (c + 1) * W)
+                    nc.vector.scalar_tensor_tensor(halves[c][:, :, t], ds[:, cols], neg_gain[:, t : t + 1], gub[:, cols], ALU.mult, ALU.add)
+            if tiles[0] == 0:
+                duo_words = keep.tile([P, S], U32, name="duo_words", tag="picked", align_bytes=64)
+                duo_plane = keep.tile([P, S], U8, name="duo_plane", align_bytes=64)
+                nc.vector.tensor_copy(duo_words[:], x_tab[:].indirect(duo_t[:]))
+                nc.vector.tensor_copy(duo_plane[:], x_bytes[:].indirect(duo_t[:]))
+                acc2 = [psum.tile([P, S], F32, name="h2_acc%d" % t) for t in range(TILES)]
+                for t in range(TILES):
+                    rows = slice(t * P, (t + 1) * P)
+                    nc.tensor.matmul_mx(
+                        out=acc2[t][:],
+                        lhsT=w2_tab[:, rows].bitcast(FP8X4),
+                        lhsT_scale=w2_plane[:, rows],
+                        rhs=duo_words[:].bitcast(FP8X4),
+                        rhs_scale=duo_plane[:],
+                        start=True,
+                        stop=False,
+                    )
+
+        for c in range(2):
+            z_words = keep.tile([P, W], U32, name="z_words%d" % c, align_bytes=64)
+            z_plane = keep.tile([P, W], U8, name="z_plane%d" % c, align_bytes=64)
+            nc.vector.quantize_mx(out=z_words[:].bitcast(FP8X4), scales=z_plane[:], in_=halves[c][:].rearrange("p w j -> p (w j)"))
+            for t in range(TILES):
+                rows = slice(t * P, (t + 1) * P)
+                nc.tensor.matmul_mx(
+                    out=acc2[t][:, c * W : (c + 1) * W],
+                    lhsT=w1_tab[:, rows].bitcast(FP8X4),
+                    lhsT_scale=w1_plane[:, rows],
+                    rhs=z_words[:].bitcast(FP8X4),
+                    rhs_scale=z_plane[:],
+                    start=False,
+                    stop=(c == 1),
+                )
+
+        h2 = []
+        for t in range(TILES):
+            h2_t = keep.tile([P, S], F32, name="h2_%d" % t)
+            if t == 0:
+                nc.scalar.activation(h2_t[:], acc2[t][:], ACT.Copy)
+            else:
+                nc.vector.tensor_copy(h2_t[:], acc2[t][:])
+            h2.append(h2_t)
+
+        ub2 = [keep.tile([P, WIDE], F32, name="ub2_%d" % t) for t in range(TILES)]
+        for t in range(TILES):
+            nc.vector.memset(ub2[t][:, S:], 0.0)
+        for tiles in ((0, 1), (2, 3)):
+            pair_up(h2, tiles, n6_t, n7_t, ALU.max, ALU.min, ub2, n8_t, n9_t, "b")
+            for t in tiles:
+                sg = keep.tile([P, S], F32, name="sg%d" % t)
+                nc.scalar.activation(sg[:], ub2[t][:].indirect(n10_t[:]), ACT.Sigmoid, bias=bias[:, t : t + 1], scale=slope[:, t : t + 1])
+                res = keep.tile([P, S], F32, name="res%d" % t)
+                nc.vector.tensor_tensor(res[:], ub2[t][:, :S], sg[:], ALU.mult)
+                nc.sync.dma_start(out[t * P : (t + 1) * P, :], res[:])

@@ -42,7 +42,7 @@ def tile_picked_mttzntcpsdeord_none_p_kernel(
             return tile
 
         def zeroed_bytes(width, name):
-            tile = keep.tile([P, width], U8, name=name, align_bytes=64)
+            tile = keep.tile([P, width], U8, name=name, tag=name, align_bytes=64)
             nc.vector.memset(tile[:].bitcast(I32), 0)
             return tile
 
@@ -51,19 +51,19 @@ def tile_picked_mttzntcpsdeord_none_p_kernel(
             for r in range(4):
                 queue.dma_start(tile[r:P:32, :].bitcast(I32), rows[r:16:4, :])
 
-        d_bytes = zeroed_bytes(G, "d_bytes")
+        d_bytes = keep.tile([P, G], U8, name="d_bytes", align_bytes=64)
         x_bytes = zeroed_bytes(T, "x_bytes")
         dk_plane = zeroed_bytes(2 * H, "dk_plane")
         k1_t = load_list(k1, "k1")
         k2_t = load_list(k2, "k2")
-        nc.scalar.dma_start(d_bytes[0:P:8, :].bitcast(I32), d_scales[0].bitcast(I32))
+        nc.scalar.dma_start(d_bytes[:].bitcast(I32), d_scales[0].bitcast(I32).unsqueeze(1).to_broadcast([16, 8, G // 4]))
         d_tab = load_words(d_words, "d_tab")
         offs_t = load_list(offs, "offs")
         two_t = load_list(two, "two")
         x_tab = load_words(x_words, "x_tab")
         load_scale_rows(x_bytes, x_scales, nc.scalar)
 
-        dk_bytes = keep.tile([P, 2 * H], U8, name="dk_bytes", align_bytes=64)
+        dk_bytes = keep.tile([P, 2 * H], U8, name="dk_bytes", tag="lhs1", align_bytes=64)
         for l, lst in enumerate((k1_t, k2_t)):
             nc.vector.tensor_copy(dk_bytes[:, l * H : (l + 1) * H], d_bytes[:].indirect(lst[:]))
         for r in range(4):
@@ -84,7 +84,7 @@ def tile_picked_mttzntcpsdeord_none_p_kernel(
 
         h = []
         for t in range(TILES):
-            lhs_words = keep.tile([P, 2, P], U32, name="lhs_words%d" % t, align_bytes=64)
+            lhs_words = keep.tile([P, 2, P], U32, name="lhs_words%d" % t, tag="lhs%d" % (t % 2), align_bytes=64)
             lhs_plane = keep.tile([P, 2, P], U8, name="lhs_plane%d" % t, align_bytes=64)
             nc.vector.tensor_copy(lhs_words[:], dk_words[:].rearrange("p (l m t) -> p t l m", l=2, t=TILES)[:, t])
             nc.vector.tensor_copy(lhs_plane[:], dk_plane[:].rearrange("p (l m t) -> p t l m", l=2, t=TILES)[:, t])
@@ -155,7 +155,7 @@ def tile_picked_mttzntcpsdeord_none_p_kernel(
                     nc.vector.scalar_tensor_tensor(halves[c][:, :, t], ds[:, cols], neg_gain[:, t : t + 1], gub[:, cols], ALU.mult, ALU.add)
             if tiles[0] == 0:
                 duo_words = keep.tile([P, S], U32, name="duo_words", tag="picked", align_bytes=64)
-                duo_plane = keep.tile([P, S], U8, name="duo_plane", align_bytes=64)
+                duo_plane = keep.tile([P, S], U8, name="duo_plane", tag="dk_plane", align_bytes=64)
                 nc.vector.tensor_copy(duo_words[:], x_tab[:].indirect(duo_t[:]))
                 nc.vector.tensor_copy(duo_plane[:], x_bytes[:].indirect(duo_t[:]))
                 acc2 = [psum.tile([P, S], F32, name="h2_acc%d" % t) for t in range(TILES)]
@@ -171,21 +171,27 @@ def tile_picked_mttzntcpsdeord_none_p_kernel(
                         stop=False,
                     )
 
+        z_words = keep.tile([P, S], U32, name="z_words", align_bytes=64)
+        z_plane = keep.tile([P, S], U8, name="z_plane", align_bytes=64)
+
+        def second_product(t, cols, stop):
+            rows = slice(t * P, (t + 1) * P)
+            nc.tensor.matmul_mx(
+                out=acc2[t][:, cols],
+                lhsT=w1_tab[:, rows].bitcast(FP8X4),
+                lhsT_scale=w1_plane[:, rows],
+                rhs=z_words[:, cols].bitcast(FP8X4),
+                rhs_scale=z_plane[:, cols],
+                start=False,
+                stop=stop,
+            )
+
         for c in range(2):
-            z_words = keep.tile([P, W], U32, name="z_words%d" % c, align_bytes=64)
-            z_plane = keep.tile([P, W], U8, name="z_plane%d" % c, align_bytes=64)
-            nc.vector.quantize_mx(out=z_words[:].bitcast(FP8X4), scales=z_plane[:], in_=halves[c][:].rearrange("p w j -> p (w j)"))
-            for t in range(TILES):
-                rows = slice(t * P, (t + 1) * P)
-                nc.tensor.matmul_mx(
-                    out=acc2[t][:, c * W : (c + 1) * W],
-                    lhsT=w1_tab[:, rows].bitcast(FP8X4),
-                    lhsT_scale=w1_plane[:, rows],
-                    rhs=z_words[:].bitcast(FP8X4),
-                    rhs_scale=z_plane[:],
-                    start=False,
-                    stop=(c == 1),
-                )
+            cols = slice(c * W, (c + 1) * W)
+            nc.vector.quantize_mx(out=z_words[:, cols].bitcast(FP8X4), scales=z_plane[:, cols], in_=halves[c][:].rearrange("p w j -> p (w j)"))
+            second_product(0, cols, c == 1)
+        for t in range(1, TILES):
+            second_product(t, slice(0, S), True)
 
         h2 = []
         for t in range(TILES):

@@ -63,6 +63,11 @@ def tile_picked_mttzntcpsdeord_none_p_kernel(
         x_tab = load_words(x_words, "x_tab")
         load_scale_rows(x_bytes, x_scales, nc.scalar)
 
+        warm_in = keep.tile([P, 1], F32, name="warm_in")
+        warm_out = keep.tile([P, 1], F32, name="warm_out")
+        nc.vector.memset(warm_in[:], 0.0)
+        nc.scalar.activation(warm_out[:], warm_in[:], ACT.Sigmoid)
+
         dk_bytes = keep.tile([P, 2 * H], U8, name="dk_bytes", tag="lhs1", align_bytes=64)
         for l, lst in enumerate((k1_t, k2_t)):
             nc.vector.tensor_copy(dk_bytes[:, l * H : (l + 1) * H], d_bytes[:].indirect(lst[:]))

@@ -87,9 +87,8 @@ def tile_picked_mttzntcpsdeord_none_p_kernel(
         gain = keep.tile([P, TILES], F32, name="gain")
         nc.sync.dma_start(gain[:], gn.rearrange("(p t) o -> p (t o)", t=TILES))
 
-        h = []
-        for t in range(TILES):
-            lhs_words = keep.tile([P, 2, P], U32, name="lhs_words%d" % t, tag="lhs%d" % (t % 2), align_bytes=64)
+        def first_product(t):
+            lhs_words = keep.tile([P, 2, P], U32, name="lhs_words%d" % t, tag=("lhs0", "lhs1", "a_pa1", "a_pb1")[t], align_bytes=64)
             lhs_plane = keep.tile([P, 2, P], U8, name="lhs_plane%d" % t, align_bytes=64)
             nc.vector.tensor_copy(lhs_words[:], dk_words[:].rearrange("p (l m t) -> p t l m", l=2, t=TILES)[:, t])
             nc.vector.tensor_copy(lhs_plane[:], dk_plane[:].rearrange("p (l m t) -> p t l m", l=2, t=TILES)[:, t])
@@ -110,7 +109,9 @@ def tile_picked_mttzntcpsdeord_none_p_kernel(
                 nc.scalar.activation(h_t[:], acc[:], ACT.Copy, scale=0.0625)
             else:
                 nc.vector.tensor_scalar(h_t[:], acc[:], 0.0625, None, ALU.mult)
-            h.append(h_t)
+            return h_t
+
+        h = {t: first_product(t) for t in (0, 1)}
 
         duo_t, n6_t, n7_t, n8_t, n9_t, n10_t = [load_list(a, nm) for a, nm in ((duo, "duo"), (n6, "n6"), (n7, "n7"), (n8, "n8"), (n9, "n9"), (n10, "n10"))]
         w2_tab = load_words(w2_words, "w2_tab")
@@ -133,8 +134,8 @@ def tile_picked_mttzntcpsdeord_none_p_kernel(
         def pair_up(src, tiles, first, second, op_a, op_b, dst, put_a, put_b, name):
             ra, rb = {}, {}
             for t in tiles:
-                pa = keep.tile([P, W], F32, name="%s_pa%d" % (name, t))
-                pb = keep.tile([P, W], F32, name="%s_pb%d" % (name, t))
+                pa = keep.tile([P, W], F32, name="%s_pa%d" % (name, t), tag="%s_pa%d" % (name, t), align_bytes=64)
+                pb = keep.tile([P, W], F32, name="%s_pb%d" % (name, t), tag="%s_pb%d" % (name, t), align_bytes=64)
                 nc.scalar.activation(pa[:], src[t][:].indirect(first[:]), ACT.Copy)
                 nc.scalar.activation(pb[:], src[t][:].indirect(second[:]), ACT.Copy)
                 ra[t] = keep.tile([P, W], F32, name="%s_ra%d" % (name, t))
@@ -150,17 +151,11 @@ def tile_picked_mttzntcpsdeord_none_p_kernel(
         ub = [keep.tile([P, S], F32, name="ub%d" % t) for t in range(TILES)]
         for tiles in ((0, 1), (2, 3)):
             pair_up(h, tiles, n1_t, n2_t, ALU.min, ALU.add, ub, n3_t, n4_t, "a")
-            for t in tiles:
-                ds = keep.tile([P, WIDE], F32, name="ds%d" % t)
-                nc.scalar.activation(ds[:].indirect(n5_t[:]), ub[t][:], ACT.Copy)
-                gub = keep.tile([P, S], F32, name="gub%d" % t)
-                nc.vector.tensor_scalar(gub[:], ub[t][:], gain[:, t : t + 1], None, ALU.mult)
-                for c in range(2):
-                    cols = slice(c * W, (c + 1) * W)
-                    nc.vector.scalar_tensor_tensor(halves[c][:, :, t], ds[:, cols], neg_gain[:, t : t + 1], gub[:, cols], ALU.mult, ALU.add)
             if tiles[0] == 0:
-                duo_words = keep.tile([P, S], U32, name="duo_words", tag="picked", align_bytes=64)
-                duo_plane = keep.tile([P, S], U8, name="duo_plane", tag="dk_plane", align_bytes=64)
+                h[2], h[3] = first_product(2), first_product(3)
+            else:
+                duo_words = keep.tile([P, S], U32, name="duo_words", tag="a_pa3", align_bytes=64)
+                duo_plane = keep.tile([P, S], U8, name="duo_plane", tag="a_pb3", align_bytes=64)
                 nc.vector.tensor_copy(duo_words[:], x_tab[:].indirect(duo_t[:]))
                 nc.vector.tensor_copy(duo_plane[:], x_bytes[:].indirect(duo_t[:]))
                 acc2 = [psum.tile([P, S], F32, name="h2_acc%d" % t) for t in range(TILES)]
@@ -175,6 +170,14 @@ def tile_picked_mttzntcpsdeord_none_p_kernel(
                         start=True,
                         stop=False,
                     )
+            for t in tiles:
+                ds = keep.tile([P, WIDE], F32, name="ds%d" % t)
+                nc.scalar.activation(ds[:].indirect(n5_t[:]), ub[t][:], ACT.Copy)
+                gub = keep.tile([P, S], F32, name="gub%d" % t)
+                nc.vector.tensor_scalar(gub[:], ub[t][:], gain[:, t : t + 1], None, ALU.mult)
+                for c in range(2):
+                    cols = slice(c * W, (c + 1) * W)
+                    nc.vector.scalar_tensor_tensor(halves[c][:, :, t], ds[:, cols], neg_gain[:, t : t + 1], gub[:, cols], ALU.mult, ALU.add)
 
         z_words = keep.tile([P, S], U32, name="z_words", align_bytes=64)
         z_plane = keep.tile([P, S], U8, name="z_plane", align_bytes=64)
@@ -213,8 +216,13 @@ def tile_picked_mttzntcpsdeord_none_p_kernel(
         for tiles in ((0, 1), (2, 3)):
             pair_up(h2, tiles, n6_t, n7_t, ALU.max, ALU.min, ub2, n8_t, n9_t, "b")
             for t in tiles:
-                sg = keep.tile([P, S], F32, name="sg%d" % t)
-                nc.scalar.activation(sg[:], ub2[t][:].indirect(n10_t[:]), ACT.Sigmoid, bias=bias[:, t : t + 1], scale=slope[:, t : t + 1])
-                res = keep.tile([P, S], F32, name="res%d" % t)
-                nc.vector.tensor_tensor(res[:], ub2[t][:, :S], sg[:], ALU.mult)
-                nc.sync.dma_start(out[t * P : (t + 1) * P, :], res[:])
+                piece = W if t == TILES - 1 else S
+                for c0 in range(0, S, piece):
+                    cols = slice(c0, c0 + piece)
+                    sg = keep.tile([P, piece], F32, name="sg%d_%d" % (t, c0))
+                    nc.scalar.activation(
+                        sg[:], ub2[t][:].indirect(n10_t[:, c0 // 16 : (c0 + piece) // 16]), ACT.Sigmoid, bias=bias[:, t : t + 1], scale=slope[:, t : t + 1]
+                    )
+                    res = keep.tile([P, piece], F32, name="res%d_%d" % (t, c0))
+                    nc.vector.tensor_tensor(res[:], ub2[t][:, cols], sg[:], ALU.mult)
+                    nc.sync.dma_start(out[t * P : (t + 1) * P, cols], res[:])

@@ -2,8 +2,8 @@ from contextlib import ExitStack
 
 import concourse.mybir as mybir
 
-K, T, S, N, G, H, W = 512, 1024, 256, 512, 2048, 512, 128
-FLOPS = 2 * 4 * 512 * 512 * 256
+T, S, N, G, H, W = 1024, 256, 512, 2048, 512, 128
+FLOPS = 4 * 2 * 512 * 512 * 256
 
 F32 = mybir.dt.float32
 BF16 = mybir.dt.bfloat16
@@ -18,7 +18,13 @@ ALU = mybir.AluOpType
 P = 128
 PACK = 4
 TILES = 4
+BLOCKS = 16
+BLOCK_PARTITIONS = 8
+QUADRANT = 32
+LIST_ROWS = 16
 WIDE = 2 * S
+PAIRS = ((0, 1), (2, 3))
+HALVES = (slice(0, W), slice(W, S))
 
 
 def tile_picked_mttzntcpsdeord_none_p_kernel(
@@ -36,31 +42,33 @@ def tile_picked_mttzntcpsdeord_none_p_kernel(
             nc.sync.dma_start(tile[:], src)
             return tile
 
-        def load_words(src, name, tag=""):
-            tile = keep.tile([P, src.shape[2]], U32, name=name, tag=tag or name, align_bytes=64)
+        def load_words(src, name):
+            tile = keep.tile([P, src.shape[2]], U32, name=name, align_bytes=64)
             nc.sync.dma_start(tile[:].bitcast(I32), src[0].rearrange("p n r -> p (n r)").bitcast(I32))
             return tile
 
-        def zeroed_bytes(width, name):
-            tile = keep.tile([P, width], U8, name=name, tag=name, align_bytes=64)
+        def zeroed_plane(width, name):
+            tile = keep.tile([P, width], U8, name=name, align_bytes=64)
             nc.vector.memset(tile[:].bitcast(I32), 0)
             return tile
 
-        def load_scale_rows(tile, src, queue):
+        def load_scale_rows(plane, src, queue):
             rows = src[0].bitcast(I32)
             for r in range(4):
-                queue.dma_start(tile[r:P:32, :].bitcast(I32), rows[r:16:4, :])
+                queue.dma_start(plane[r:P:QUADRANT, :].bitcast(I32), rows[r:BLOCKS:4, :])
 
-        d_bytes = keep.tile([P, G], U8, name="d_bytes", align_bytes=64)
-        x_bytes = zeroed_bytes(T, "x_bytes")
-        dk_plane = zeroed_bytes(2 * H, "dk_plane")
+        x_bytes = zeroed_plane(T, "x_bytes")
+        code_plane = zeroed_plane(2 * H, "code_plane")
         k1_t = load_list(k1, "k1")
         k2_t = load_list(k2, "k2")
-        nc.scalar.dma_start(d_bytes[:].bitcast(I32), d_scales[0].bitcast(I32).unsqueeze(1).to_broadcast([16, 8, G // 4]))
-        d_tab = load_words(d_words, "d_tab")
+        d_bytes = keep.tile([P, G], U8, name="d_bytes", align_bytes=64)
+        nc.scalar.dma_start(
+            d_bytes[:].bitcast(I32), d_scales[0].bitcast(I32).unsqueeze(1).to_broadcast([BLOCKS, BLOCK_PARTITIONS, G // 4])
+        )
+        d_table = load_words(d_words, "d_table")
         offs_t = load_list(offs, "offs")
         two_t = load_list(two, "two")
-        x_tab = load_words(x_words, "x_tab")
+        x_table = load_words(x_words, "x_table")
         load_scale_rows(x_bytes, x_scales, nc.scalar)
 
         warm_in = keep.tile([P, 1], F32, name="warm_in")
@@ -68,39 +76,42 @@ def tile_picked_mttzntcpsdeord_none_p_kernel(
         nc.vector.memset(warm_in[:], 0.0)
         nc.scalar.activation(warm_out[:], warm_in[:], ACT.Sigmoid)
 
-        dk_bytes = keep.tile([P, 2 * H], U8, name="dk_bytes", tag="lhs1", align_bytes=64)
+        code_bytes = keep.tile([P, 2 * H], U8, name="code_bytes", tag="code_bytes", align_bytes=64)
         for l, lst in enumerate((k1_t, k2_t)):
-            nc.vector.tensor_copy(dk_bytes[:, l * H : (l + 1) * H], d_bytes[:].indirect(lst[:]))
+            nc.vector.tensor_copy(code_bytes[:, l * H : (l + 1) * H], d_bytes[:].indirect(lst[:]))
         for r in range(4):
-            nc.scalar.dma_start(dk_plane[r:P:32, :].bitcast(I32), dk_bytes[8 * r : P : 32, :].bitcast(I32))
-        dk_words = keep.tile([P, 2 * H], U32, name="dk_words", tag="picked", align_bytes=64)
+            nc.scalar.dma_start(
+                code_plane[r:P:QUADRANT, :].bitcast(I32), code_bytes[BLOCK_PARTITIONS * r : P : QUADRANT, :].bitcast(I32)
+            )
+        code_words = keep.tile([P, 2 * H], U32, name="code_words", align_bytes=64)
         for l, lst in enumerate((k1_t, k2_t)):
-            nc.vector.tensor_copy(dk_words[:, l * H : (l + 1) * H], d_tab[:].indirect(lst[:]))
-        xq_words = keep.tile([P, 2 * S], U32, name="xq_words", align_bytes=64)
-        xq_plane = keep.tile([P, 2 * S], U8, name="xq_plane", align_bytes=64)
+            nc.vector.tensor_copy(code_words[:, l * H : (l + 1) * H], d_table[:].indirect(lst[:]))
+        token_words = keep.tile([P, 2 * S], U32, name="token_words", align_bytes=64)
+        token_plane = keep.tile([P, 2 * S], U8, name="token_plane", align_bytes=64)
         for l, lst in enumerate((offs_t, two_t)):
-            nc.vector.tensor_copy(xq_words[:, l * S : (l + 1) * S], x_tab[:].indirect(lst[:]))
+            nc.vector.tensor_copy(token_words[:, l * S : (l + 1) * S], x_table[:].indirect(lst[:]))
         for l, lst in enumerate((offs_t, two_t)):
-            nc.vector.tensor_copy(xq_plane[:, l * S : (l + 1) * S], x_bytes[:].indirect(lst[:]))
+            nc.vector.tensor_copy(token_plane[:, l * S : (l + 1) * S], x_bytes[:].indirect(lst[:]))
 
         n1_t, n2_t, n3_t, n4_t, n5_t = [load_list(a, nm) for a, nm in ((n1, "n1"), (n2, "n2"), (n3, "n3"), (n4, "n4"), (n5, "n5"))]
         gain = keep.tile([P, TILES], F32, name="gain")
         nc.sync.dma_start(gain[:], gn.rearrange("(p t) o -> p (t o)", t=TILES))
 
-        def first_product(t):
-            lhs_words = keep.tile([P, 2, P], U32, name="lhs_words%d" % t, tag=("lhs0", "lhs1", "a_pa1", "a_pb1")[t], align_bytes=64)
+        def first_product(t, words_tag):
+            dealt = "p (l m t) -> p t l m"
+            lhs_words = keep.tile([P, 2, P], U32, name="lhs_words%d" % t, tag=words_tag, align_bytes=64)
             lhs_plane = keep.tile([P, 2, P], U8, name="lhs_plane%d" % t, align_bytes=64)
-            nc.vector.tensor_copy(lhs_words[:], dk_words[:].rearrange("p (l m t) -> p t l m", l=2, t=TILES)[:, t])
-            nc.vector.tensor_copy(lhs_plane[:], dk_plane[:].rearrange("p (l m t) -> p t l m", l=2, t=TILES)[:, t])
-            acc = psum.tile([P, S], F32, name="h_acc%d" % t)
+            nc.vector.tensor_copy(lhs_words[:], code_words[:].rearrange(dealt, l=2, t=TILES)[:, t])
+            nc.vector.tensor_copy(lhs_plane[:], code_plane[:].rearrange(dealt, l=2, t=TILES)[:, t])
+            acc = psum.tile([P, S], F32, name="h_acc%d" % t, tag="h_acc%d" % t)
             for l in range(2):
                 cols = slice(l * S, (l + 1) * S)
                 nc.tensor.matmul_mx(
                     out=acc[:],
                     lhsT=lhs_words[:, l, :].bitcast(FP8X4),
                     lhsT_scale=lhs_plane[:, l, :],
-                    rhs=xq_words[:, cols].bitcast(FP8X4),
-                    rhs_scale=xq_plane[:, cols],
+                    rhs=token_words[:, cols].bitcast(FP8X4),
+                    rhs_scale=token_plane[:, cols],
                     start=(l == 0),
                     stop=(l == 1),
                 )
@@ -111,13 +122,15 @@ def tile_picked_mttzntcpsdeord_none_p_kernel(
                 nc.vector.tensor_scalar(h_t[:], acc[:], 0.0625, None, ALU.mult)
             return h_t
 
-        h = {t: first_product(t) for t in (0, 1)}
+        h = {0: first_product(0, "lhs_words0"), 1: first_product(1, "code_bytes")}
 
-        duo_t, n6_t, n7_t, n8_t, n9_t, n10_t = [load_list(a, nm) for a, nm in ((duo, "duo"), (n6, "n6"), (n7, "n7"), (n8, "n8"), (n9, "n9"), (n10, "n10"))]
-        w2_tab = load_words(w2_words, "w2_tab")
-        w1_tab = load_words(w1_words, "w1_tab")
-        w2_plane = zeroed_bytes(N, "w2_plane")
-        w1_plane = zeroed_bytes(N, "w1_plane")
+        duo_t, n6_t, n7_t, n8_t, n9_t, n10_t = [
+            load_list(a, nm) for a, nm in ((duo, "duo"), (n6, "n6"), (n7, "n7"), (n8, "n8"), (n9, "n9"), (n10, "n10"))
+        ]
+        w2_table = load_words(w2_words, "w2_table")
+        w1_table = load_words(w1_words, "w1_table")
+        w2_plane = zeroed_plane(N, "w2_plane")
+        w1_plane = zeroed_plane(N, "w1_plane")
         load_scale_rows(w2_plane, w2_scales, nc.sync)
         load_scale_rows(w1_plane, w1_scales, nc.sync)
         slope = keep.tile([P, TILES], F32, name="slope")
@@ -131,15 +144,15 @@ def tile_picked_mttzntcpsdeord_none_p_kernel(
         bias = keep.tile([P, TILES], F32, name="bias")
         nc.vector.scalar_tensor_tensor(bias[:], slope[:], -1.0, thresh[:], ALU.mult, ALU.mult)
 
-        def pair_up(src, tiles, first, second, op_a, op_b, dst, put_a, put_b, name):
+        def pair_up(src, tiles, get_a, get_b, op_a, op_b, dst, put_a, put_b, step):
             ra, rb = {}, {}
             for t in tiles:
-                pa = keep.tile([P, W], F32, name="%s_pa%d" % (name, t), tag="%s_pa%d" % (name, t), align_bytes=64)
-                pb = keep.tile([P, W], F32, name="%s_pb%d" % (name, t), tag="%s_pb%d" % (name, t), align_bytes=64)
-                nc.scalar.activation(pa[:], src[t][:].indirect(first[:]), ACT.Copy)
-                nc.scalar.activation(pb[:], src[t][:].indirect(second[:]), ACT.Copy)
-                ra[t] = keep.tile([P, W], F32, name="%s_ra%d" % (name, t))
-                rb[t] = keep.tile([P, W], F32, name="%s_rb%d" % (name, t))
+                pa = keep.tile([P, W], F32, name="%s_pa%d" % (step, t), tag="%s_pa%d" % (step, t), align_bytes=64)
+                pb = keep.tile([P, W], F32, name="%s_pb%d" % (step, t), tag="%s_pb%d" % (step, t), align_bytes=64)
+                nc.scalar.activation(pa[:], src[t][:].indirect(get_a[:]), ACT.Copy)
+                nc.scalar.activation(pb[:], src[t][:].indirect(get_b[:]), ACT.Copy)
+                ra[t] = keep.tile([P, W], F32, name="%s_ra%d" % (step, t))
+                rb[t] = keep.tile([P, W], F32, name="%s_rb%d" % (step, t))
                 nc.vector.tensor_tensor(ra[t][:], pa[:], pb[:], op_a)
                 nc.vector.tensor_tensor(rb[t][:], pa[:], pb[:], op_b)
             for t in tiles:
@@ -147,82 +160,85 @@ def tile_picked_mttzntcpsdeord_none_p_kernel(
             for t in tiles:
                 nc.scalar.activation(dst[t][:].indirect(put_b[:]), rb[t][:], ACT.Copy)
 
-        halves = [keep.tile([P, W, PACK], BF16, name="z_half%d" % c, align_bytes=64) for c in range(2)]
+        z_rounded = [keep.tile([P, W, PACK], BF16, name="z_rounded%d" % c, align_bytes=64) for c in range(2)]
         ub = [keep.tile([P, S], F32, name="ub%d" % t) for t in range(TILES)]
-        for tiles in ((0, 1), (2, 3)):
-            pair_up(h, tiles, n1_t, n2_t, ALU.min, ALU.add, ub, n3_t, n4_t, "a")
-            if tiles[0] == 0:
-                h[2], h[3] = first_product(2), first_product(3)
-            else:
-                duo_words = keep.tile([P, S], U32, name="duo_words", tag="a_pa3", align_bytes=64)
-                duo_plane = keep.tile([P, S], U8, name="duo_plane", tag="a_pb3", align_bytes=64)
-                nc.vector.tensor_copy(duo_words[:], x_tab[:].indirect(duo_t[:]))
-                nc.vector.tensor_copy(duo_plane[:], x_bytes[:].indirect(duo_t[:]))
-                acc2 = [psum.tile([P, S], F32, name="h2_acc%d" % t) for t in range(TILES)]
-                for t in range(TILES):
-                    rows = slice(t * P, (t + 1) * P)
-                    nc.tensor.matmul_mx(
-                        out=acc2[t][:],
-                        lhsT=w2_tab[:, rows].bitcast(FP8X4),
-                        lhsT_scale=w2_plane[:, rows],
-                        rhs=duo_words[:].bitcast(FP8X4),
-                        rhs_scale=duo_plane[:],
-                        start=True,
-                        stop=False,
-                    )
+
+        def make_z(tiles):
             for t in tiles:
                 ds = keep.tile([P, WIDE], F32, name="ds%d" % t)
                 nc.scalar.activation(ds[:].indirect(n5_t[:]), ub[t][:], ACT.Copy)
-                gub = keep.tile([P, S], F32, name="gub%d" % t)
-                nc.vector.tensor_scalar(gub[:], ub[t][:], gain[:, t : t + 1], None, ALU.mult)
-                for c in range(2):
-                    cols = slice(c * W, (c + 1) * W)
-                    nc.vector.scalar_tensor_tensor(halves[c][:, :, t], ds[:, cols], neg_gain[:, t : t + 1], gub[:, cols], ALU.mult, ALU.add)
+                scaled_ub = keep.tile([P, S], F32, name="scaled_ub%d" % t)
+                nc.vector.tensor_scalar(scaled_ub[:], ub[t][:], gain[:, t : t + 1], None, ALU.mult)
+                for c, cols in enumerate(HALVES):
+                    nc.vector.scalar_tensor_tensor(
+                        z_rounded[c][:, :, t], ds[:, cols], neg_gain[:, t : t + 1], scaled_ub[:, cols], ALU.mult, ALU.add
+                    )
+
+        pair_up(h, PAIRS[0], n1_t, n2_t, ALU.min, ALU.add, ub, n3_t, n4_t, "first")
+        h[2], h[3] = first_product(2, "first_pa1"), first_product(3, "first_pb1")
+        make_z(PAIRS[0])
+        pair_up(h, PAIRS[1], n1_t, n2_t, ALU.min, ALU.add, ub, n3_t, n4_t, "first")
+        duo_words = keep.tile([P, S], U32, name="duo_words", tag="first_pa3", align_bytes=64)
+        duo_plane = keep.tile([P, S], U8, name="duo_plane", tag="first_pb3", align_bytes=64)
+        nc.vector.tensor_copy(duo_words[:], x_table[:].indirect(duo_t[:]))
+        nc.vector.tensor_copy(duo_plane[:], x_bytes[:].indirect(duo_t[:]))
+
+        groups = [(0, cols) for cols in HALVES] + [(t, slice(0, S)) for t in range(1, TILES)]
+        h2_acc = []
+        for i, (t, cols) in enumerate(groups):
+            rows = slice(t * P, (t + 1) * P)
+            h2_acc.append(psum.tile([P, cols.stop - cols.start], F32, name="h2_acc%d" % i, tag="h_acc0" if i == 0 else "h2_acc%d" % i))
+            nc.tensor.matmul_mx(
+                out=h2_acc[i][:],
+                lhsT=w2_table[:, rows].bitcast(FP8X4),
+                lhsT_scale=w2_plane[:, rows],
+                rhs=duo_words[:, cols].bitcast(FP8X4),
+                rhs_scale=duo_plane[:, cols],
+                start=True,
+                stop=False,
+            )
+        make_z(PAIRS[1])
 
         z_words = keep.tile([P, S], U32, name="z_words", align_bytes=64)
         z_plane = keep.tile([P, S], U8, name="z_plane", align_bytes=64)
+        for c, cols in enumerate(HALVES):
+            nc.vector.quantize_mx(
+                out=z_words[:, cols].bitcast(FP8X4), scales=z_plane[:, cols], in_=z_rounded[c][:].rearrange("p w j -> p (w j)")
+            )
 
-        def second_product(t, cols, stop):
+        h2 = [keep.tile([P, S], F32, name="h2_%d" % t) for t in range(TILES)]
+        for i, (t, cols) in enumerate(groups):
             rows = slice(t * P, (t + 1) * P)
             nc.tensor.matmul_mx(
-                out=acc2[t][:, cols],
-                lhsT=w1_tab[:, rows].bitcast(FP8X4),
+                out=h2_acc[i][:],
+                lhsT=w1_table[:, rows].bitcast(FP8X4),
                 lhsT_scale=w1_plane[:, rows],
                 rhs=z_words[:, cols].bitcast(FP8X4),
                 rhs_scale=z_plane[:, cols],
                 start=False,
-                stop=stop,
+                stop=True,
             )
-
-        for c in range(2):
-            cols = slice(c * W, (c + 1) * W)
-            nc.vector.quantize_mx(out=z_words[:, cols].bitcast(FP8X4), scales=z_plane[:, cols], in_=halves[c][:].rearrange("p w j -> p (w j)"))
-            second_product(0, cols, c == 1)
-        for t in range(1, TILES):
-            second_product(t, slice(0, S), True)
-
-        h2 = []
-        for t in range(TILES):
-            h2_t = keep.tile([P, S], F32, name="h2_%d" % t)
             if t == 0:
-                nc.scalar.activation(h2_t[:], acc2[t][:], ACT.Copy)
+                nc.scalar.activation(h2[t][:, cols], h2_acc[i][:], ACT.Copy)
             else:
-                nc.vector.tensor_copy(h2_t[:], acc2[t][:])
-            h2.append(h2_t)
+                nc.vector.tensor_copy(h2[t][:, cols], h2_acc[i][:])
 
         ub2 = [keep.tile([P, WIDE], F32, name="ub2_%d" % t) for t in range(TILES)]
         for t in range(TILES):
             nc.vector.memset(ub2[t][:, S:], 0.0)
-        for tiles in ((0, 1), (2, 3)):
-            pair_up(h2, tiles, n6_t, n7_t, ALU.max, ALU.min, ub2, n8_t, n9_t, "b")
+        for tiles in PAIRS:
+            pair_up(h2, tiles, n6_t, n7_t, ALU.max, ALU.min, ub2, n8_t, n9_t, "last")
             for t in tiles:
-                piece = W if t == TILES - 1 else S
-                for c0 in range(0, S, piece):
-                    cols = slice(c0, c0 + piece)
-                    sg = keep.tile([P, piece], F32, name="sg%d_%d" % (t, c0))
+                for cols in HALVES if t == TILES - 1 else (slice(0, S),):
+                    width = cols.stop - cols.start
+                    sg = keep.tile([P, width], F32, name="sg%d_%d" % (t, cols.start))
                     nc.scalar.activation(
-                        sg[:], ub2[t][:].indirect(n10_t[:, c0 // 16 : (c0 + piece) // 16]), ACT.Sigmoid, bias=bias[:, t : t + 1], scale=slope[:, t : t + 1]
+                        sg[:],
+                        ub2[t][:].indirect(n10_t[:, cols.start // LIST_ROWS : cols.stop // LIST_ROWS]),
+                        ACT.Sigmoid,
+                        bias=bias[:, t : t + 1],
+                        scale=slope[:, t : t + 1],
                     )
-                    res = keep.tile([P, piece], F32, name="res%d_%d" % (t, c0))
-                    nc.vector.tensor_tensor(res[:], ub2[t][:, cols], sg[:], ALU.mult)
-                    nc.sync.dma_start(out[t * P : (t + 1) * P, cols], res[:])
+                    result = keep.tile([P, width], F32, name="result%d_%d" % (t, cols.start))
+                    nc.vector.tensor_tensor(result[:], ub2[t][:, cols], sg[:], ALU.mult)
+                    nc.sync.dma_start(out[t * P : (t + 1) * P, cols], result[:])

from contextlib import ExitStack

import concourse.mybir as mybir

T, S, N, G, H, W = 1024, 256, 512, 2048, 512, 128
FLOPS = 4 * 2 * 512 * 512 * 256

F32 = mybir.dt.float32
BF16 = mybir.dt.bfloat16
I32 = mybir.dt.int32
U32 = mybir.dt.uint32
U16 = mybir.dt.uint16
U8 = mybir.dt.uint8
FP8X4 = mybir.dt.float8_e4m3fn_x4
ACT = mybir.ActivationFunctionType
ALU = mybir.AluOpType

P = 128
PACK = 4
TILES = 4
BLOCKS = 16
BLOCK_PARTITIONS = 8
QUADRANT = 32
LIST_ROWS = 16
WIDE = 2 * S
PAIRS = ((0, 1), (2, 3))
HALVES = (slice(0, W), slice(W, S))


def tile_picked_mttzntcpsdeord_none_p_kernel(
    tc, x_words, x_scales, d_words, d_scales, gn, w1_words, w1_scales, w2_words, w2_scales, sl, th,
    offs, k1, two, k2, n1, n2, n3, n4, n5, duo, n6, n7, n8, n9, n10, out,
):
    nc = tc.nc

    with ExitStack() as ctx:
        keep = ctx.enter_context(tc.tile_pool(name="keep", bufs=1))
        psum = ctx.enter_context(tc.psum_pool(name="psum", bufs=1))

        def load_list(src, name):
            tile = keep.tile(list(src.shape), U16, name=name)
            nc.sync.dma_start(tile[:], src)
            return tile

        def load_words(src, name):
            tile = keep.tile([P, src.shape[2]], U32, name=name, align_bytes=64)
            nc.sync.dma_start(tile[:].bitcast(I32), src[0].rearrange("p n r -> p (n r)").bitcast(I32))
            return tile

        def zeroed_plane(width, name):
            tile = keep.tile([P, width], U8, name=name, align_bytes=64)
            nc.vector.memset(tile[:].bitcast(I32), 0)
            return tile

        def load_scale_rows(plane, src, queue):
            rows = src[0].bitcast(I32)
            for r in range(4):
                queue.dma_start(plane[r:P:QUADRANT, :].bitcast(I32), rows[r:BLOCKS:4, :])

        x_bytes = zeroed_plane(T, "x_bytes")
        code_plane = zeroed_plane(2 * H, "code_plane")
        k1_t = load_list(k1, "k1")
        k2_t = load_list(k2, "k2")
        d_bytes = keep.tile([P, G], U8, name="d_bytes", align_bytes=64)
        nc.scalar.dma_start(
            d_bytes[:].bitcast(I32), d_scales[0].bitcast(I32).unsqueeze(1).to_broadcast([BLOCKS, BLOCK_PARTITIONS, G // 4])
        )
        d_table = load_words(d_words, "d_table")
        offs_t = load_list(offs, "offs")
        two_t = load_list(two, "two")
        x_table = load_words(x_words, "x_table")
        load_scale_rows(x_bytes, x_scales, nc.scalar)

        warm_in = keep.tile([P, 1], F32, name="warm_in")
        warm_out = keep.tile([P, 1], F32, name="warm_out")
        nc.vector.memset(warm_in[:], 0.0)
        nc.scalar.activation(warm_out[:], warm_in[:], ACT.Sigmoid)

        code_bytes = keep.tile([P, 2 * H], U8, name="code_bytes", tag="code_bytes", align_bytes=64)
        for l, lst in enumerate((k1_t, k2_t)):
            nc.vector.tensor_copy(code_bytes[:, l * H : (l + 1) * H], d_bytes[:].indirect(lst[:]))
        for r in range(4):
            nc.scalar.dma_start(
                code_plane[r:P:QUADRANT, :].bitcast(I32), code_bytes[BLOCK_PARTITIONS * r : P : QUADRANT, :].bitcast(I32)
            )
        code_words = keep.tile([P, 2 * H], U32, name="code_words", align_bytes=64)
        for l, lst in enumerate((k1_t, k2_t)):
            nc.vector.tensor_copy(code_words[:, l * H : (l + 1) * H], d_table[:].indirect(lst[:]))
        token_words = keep.tile([P, 2 * S], U32, name="token_words", align_bytes=64)
        token_plane = keep.tile([P, 2 * S], U8, name="token_plane", align_bytes=64)
        for l, lst in enumerate((offs_t, two_t)):
            nc.vector.tensor_copy(token_words[:, l * S : (l + 1) * S], x_table[:].indirect(lst[:]))
        for l, lst in enumerate((offs_t, two_t)):
            nc.vector.tensor_copy(token_plane[:, l * S : (l + 1) * S], x_bytes[:].indirect(lst[:]))

        n1_t, n2_t, n3_t, n4_t, n5_t = [load_list(a, nm) for a, nm in ((n1, "n1"), (n2, "n2"), (n3, "n3"), (n4, "n4"), (n5, "n5"))]
        gain = keep.tile([P, TILES], F32, name="gain")
        nc.sync.dma_start(gain[:], gn.rearrange("(p t) o -> p (t o)", t=TILES))

        def first_product(t, words_tag):
            dealt = "p (l m t) -> p t l m"
            lhs_words = keep.tile([P, 2, P], U32, name="lhs_words%d" % t, tag=words_tag, align_bytes=64)
            lhs_plane = keep.tile([P, 2, P], U8, name="lhs_plane%d" % t, align_bytes=64)
            nc.vector.tensor_copy(lhs_words[:], code_words[:].rearrange(dealt, l=2, t=TILES)[:, t])
            nc.vector.tensor_copy(lhs_plane[:], code_plane[:].rearrange(dealt, l=2, t=TILES)[:, t])
            acc = psum.tile([P, S], F32, name="h_acc%d" % t, tag="h_acc%d" % t)
            for l in range(2):
                cols = slice(l * S, (l + 1) * S)
                nc.tensor.matmul_mx(
                    out=acc[:],
                    lhsT=lhs_words[:, l, :].bitcast(FP8X4),
                    lhsT_scale=lhs_plane[:, l, :],
                    rhs=token_words[:, cols].bitcast(FP8X4),
                    rhs_scale=token_plane[:, cols],
                    start=(l == 0),
                    stop=(l == 1),
                )
            h_t = keep.tile([P, S], F32, name="h%d" % t)
            if t == 0:
                nc.scalar.activation(h_t[:], acc[:], ACT.Copy, scale=0.0625)
            else:
                nc.vector.tensor_scalar(h_t[:], acc[:], 0.0625, None, ALU.mult)
            return h_t

        h = {0: first_product(0, "lhs_words0"), 1: first_product(1, "code_bytes")}

        duo_t, n6_t, n7_t, n8_t, n9_t, n10_t = [
            load_list(a, nm) for a, nm in ((duo, "duo"), (n6, "n6"), (n7, "n7"), (n8, "n8"), (n9, "n9"), (n10, "n10"))
        ]
        w2_table = load_words(w2_words, "w2_table")
        w1_table = load_words(w1_words, "w1_table")
        w2_plane = zeroed_plane(N, "w2_plane")
        w1_plane = zeroed_plane(N, "w1_plane")
        load_scale_rows(w2_plane, w2_scales, nc.sync)
        load_scale_rows(w1_plane, w1_scales, nc.sync)
        slope = keep.tile([P, TILES], F32, name="slope")
        thresh = keep.tile([P, TILES], F32, name="thresh")
        with nc.allow_non_contiguous_dma(reason="one value a row"):
            nc.sync.dma_start(slope[:], sl.rearrange("(t p) o -> p (t o)", t=TILES))
            nc.sync.dma_start(thresh[:], th.rearrange("(t p) o -> p (t o)", t=TILES))

        neg_gain = keep.tile([P, TILES], F32, name="neg_gain")
        nc.vector.tensor_scalar(neg_gain[:], gain[:], -1.0, None, ALU.mult)
        bias = keep.tile([P, TILES], F32, name="bias")
        nc.vector.scalar_tensor_tensor(bias[:], slope[:], -1.0, thresh[:], ALU.mult, ALU.mult)

        def pair_up(src, tiles, get_a, get_b, op_a, op_b, dst, put_a, put_b, step):
            ra, rb = {}, {}
            for t in tiles:
                pa = keep.tile([P, W], F32, name="%s_pa%d" % (step, t), tag="%s_pa%d" % (step, t), align_bytes=64)
                pb = keep.tile([P, W], F32, name="%s_pb%d" % (step, t), tag="%s_pb%d" % (step, t), align_bytes=64)
                nc.scalar.activation(pa[:], src[t][:].indirect(get_a[:]), ACT.Copy)
                nc.scalar.activation(pb[:], src[t][:].indirect(get_b[:]), ACT.Copy)
                ra[t] = keep.tile([P, W], F32, name="%s_ra%d" % (step, t))
                rb[t] = keep.tile([P, W], F32, name="%s_rb%d" % (step, t))
                nc.vector.tensor_tensor(ra[t][:], pa[:], pb[:], op_a)
                nc.vector.tensor_tensor(rb[t][:], pa[:], pb[:], op_b)
            for t in tiles:
                nc.scalar.activation(dst[t][:].indirect(put_a[:]), ra[t][:], ACT.Copy)
            for t in tiles:
                nc.scalar.activation(dst[t][:].indirect(put_b[:]), rb[t][:], ACT.Copy)

        z_rounded = [keep.tile([P, W, PACK], BF16, name="z_rounded%d" % c, align_bytes=64) for c in range(2)]
        ub = [keep.tile([P, S], F32, name="ub%d" % t) for t in range(TILES)]

        def make_z(tiles):
            for t in tiles:
                ds = keep.tile([P, WIDE], F32, name="ds%d" % t)
                nc.scalar.activation(ds[:].indirect(n5_t[:]), ub[t][:], ACT.Copy)
                scaled_ub = keep.tile([P, S], F32, name="scaled_ub%d" % t)
                nc.vector.tensor_scalar(scaled_ub[:], ub[t][:], gain[:, t : t + 1], None, ALU.mult)
                for c, cols in enumerate(HALVES):
                    nc.vector.scalar_tensor_tensor(
                        z_rounded[c][:, :, t], ds[:, cols], neg_gain[:, t : t + 1], scaled_ub[:, cols], ALU.mult, ALU.add
                    )

        pair_up(h, PAIRS[0], n1_t, n2_t, ALU.min, ALU.add, ub, n3_t, n4_t, "first")
        h[2], h[3] = first_product(2, "first_pa1"), first_product(3, "first_pb1")
        make_z(PAIRS[0])
        pair_up(h, PAIRS[1], n1_t, n2_t, ALU.min, ALU.add, ub, n3_t, n4_t, "first")
        duo_words = keep.tile([P, S], U32, name="duo_words", tag="first_pa3", align_bytes=64)
        duo_plane = keep.tile([P, S], U8, name="duo_plane", tag="first_pb3", align_bytes=64)
        nc.vector.tensor_copy(duo_words[:], x_table[:].indirect(duo_t[:]))
        nc.vector.tensor_copy(duo_plane[:], x_bytes[:].indirect(duo_t[:]))

        groups = [(0, cols) for cols in HALVES] + [(t, slice(0, S)) for t in range(1, TILES)]
        h2_acc = []
        for i, (t, cols) in enumerate(groups):
            rows = slice(t * P, (t + 1) * P)
            h2_acc.append(psum.tile([P, cols.stop - cols.start], F32, name="h2_acc%d" % i, tag="h_acc0" if i == 0 else "h2_acc%d" % i))
            nc.tensor.matmul_mx(
                out=h2_acc[i][:],
                lhsT=w2_table[:, rows].bitcast(FP8X4),
                lhsT_scale=w2_plane[:, rows],
                rhs=duo_words[:, cols].bitcast(FP8X4),
                rhs_scale=duo_plane[:, cols],
                start=True,
                stop=False,
            )
        make_z(PAIRS[1])

        z_words = keep.tile([P, S], U32, name="z_words", align_bytes=64)
        z_plane = keep.tile([P, S], U8, name="z_plane", align_bytes=64)
        for c, cols in enumerate(HALVES):
            nc.vector.quantize_mx(
                out=z_words[:, cols].bitcast(FP8X4), scales=z_plane[:, cols], in_=z_rounded[c][:].rearrange("p w j -> p (w j)")
            )

        h2 = [keep.tile([P, S], F32, name="h2_%d" % t) for t in range(TILES)]
        for i, (t, cols) in enumerate(groups):
            rows = slice(t * P, (t + 1) * P)
            nc.tensor.matmul_mx(
                out=h2_acc[i][:],
                lhsT=w1_table[:, rows].bitcast(FP8X4),
                lhsT_scale=w1_plane[:, rows],
                rhs=z_words[:, cols].bitcast(FP8X4),
                rhs_scale=z_plane[:, cols],
                start=False,
                stop=True,
            )
            if t == 0:
                nc.scalar.activation(h2[t][:, cols], h2_acc[i][:], ACT.Copy)
            else:
                nc.vector.tensor_copy(h2[t][:, cols], h2_acc[i][:])

        ub2 = [keep.tile([P, WIDE], F32, name="ub2_%d" % t) for t in range(TILES)]
        for t in range(TILES):
            nc.vector.memset(ub2[t][:, S:], 0.0)
        for tiles in PAIRS:
            pair_up(h2, tiles, n6_t, n7_t, ALU.max, ALU.min, ub2, n8_t, n9_t, "last")
            for t in tiles:
                for cols in HALVES if t == TILES - 1 else (slice(0, S),):
                    width = cols.stop - cols.start
                    sg = keep.tile([P, width], F32, name="sg%d_%d" % (t, cols.start))
                    nc.scalar.activation(
                        sg[:],
                        ub2[t][:].indirect(n10_t[:, cols.start // LIST_ROWS : cols.stop // LIST_ROWS]),
                        ACT.Sigmoid,
                        bias=bias[:, t : t + 1],
                        scale=slope[:, t : t + 1],
                    )
                    result = keep.tile([P, width], F32, name="result%d_%d" % (t, cols.start))
                    nc.vector.tensor_tensor(result[:], ub2[t][:, cols], sg[:], ALU.mult)
                    nc.sync.dma_start(out[t * P : (t + 1) * P, cols], result[:])
